import numpy as np, ml_dtypes
CORES = [44,45,46,47,172,173,174,175,300,301,302,303,428,429,430,431]
N = 16
DEG, TK, TIMES = 4, 64, 3
MASK = [[0,2,4,9],[1,2,6,15],[2,7,8,9],[0,3,7,10],[2,4,6,8],[2,4,5,12],[0,6,7,11],[5,7,10,12],[1,5,8,13],[3,8,9,14],[0,5,8,10],[0,7,11,15],[7,8,12,15],[8,11,12,13],[7,8,10,14],[0,7,11,15]]
def setup_inputs(rng):
    return {"x": rng.standard_normal((N, 128, TK), dtype=np.float32).astype(ml_dtypes.bfloat16), "w": (rng.standard_normal((N, 128, DEG * 128), dtype=np.float32) / np.float32(np.sqrt(128 * DEG / 2))).astype(ml_dtypes.bfloat16)}
def setup_inputs_big(rng):
    d = setup_inputs(rng)
    for k in ("x", "w"): d[k] = (d[k].astype(np.float32) * 1024.0).astype(d[k].dtype)
    return d
def setup_inputs_small(rng):
    d = setup_inputs(rng)
    for k in ("x", "w"): d[k] = (d[k].astype(np.float32) * (1 / 1024.0)).astype(d[k].dtype)
    return d
def setup_inputs_apart(rng):
    d = setup_inputs(rng)
    f = (10.0 ** rng.permutation(np.linspace(-1.5, 1.5, N))).astype(np.float32).reshape(N, 1, 1)
    for k in ("x", "w"): d[k] = (d[k].astype(np.float32) * f).astype(d[k].dtype)
    return d
def reference(x, w):
    X, W = x.astype(np.float64), w.astype(np.float64)
    h = list(X)
    for _ in range(TIMES):
        h = [np.maximum(sum(W[r][:, 128 * i:128 * i + 128].T @ h[j] for i, j in enumerate(MASK[r])), 0.0) for r in range(N)]
    return {"y": np.stack(h).astype(ml_dtypes.bfloat16)}

@@ -1,0 +1,277 @@
+from concourse.bass import DstId, RemoteDMATransfer
+from concourse.mybir import AluOpType
+
+PART, TK, DEG, TIMES, NR = 128, 64, 4, 3, 16
+LEVELS = (1, 2)
+NB = 2
+NLAND = 16
+
+SCRATCH = {
+    "hb": ("sbuf", [PART, (1 + TIMES * NB) * TK], "bfloat16"),
+    "ws": ("sbuf", [PART, NB * DEG * PART], "bfloat16"),
+    "land": ("sbuf", [PART, NLAND * TK], "bfloat16"),
+    "zero": ("sbuf", [PART, TK], "float32"),
+    "acc0": ("psum", [PART, 512], "float32"),
+    "acc1": ("psum", [PART, 512], "float32"),
+}
+SEMAPHORES = (["xl", "wl", "zs", "sent", "st"]
+              + ["m%d_%d" % (t, b) for t in range(1, TIMES + 1) for b in range(NB)]
+              + ["r%d_%d" % (t, b) for t in range(1, TIMES + 1) for b in range(NB)]
+              + ["a%d_%d" % (t, j) for t in range(TIMES) for j in range(NR)]
+              + ["wa%d" % j for j in range(NR)])
+
+_CACHE = {}
+
+
+def _bits(m):
+    return [e for e in range(m.bit_length()) if (m >> e) & 1]
+
+
+def _plan(cores, tab, topo):
+    n = len(cores)
+
+    def adj(a, b):
+        return a != b and topo.may_write(cores[a], cores[b])
+
+    def near(a, b):
+        return topo.host(cores[a]) == topo.host(cores[b]) and topo.chip(cores[a]) == topo.chip(cores[b])
+
+    def engines(a, b):
+        narrow = 0
+        for c in range(n):
+            if adj(a, c):
+                m = topo.mask(cores[a], cores[c])
+                narrow = m if narrow == 0 else narrow & m
+        m = topo.mask(cores[a], cores[b])
+        if m != narrow and m & ~narrow:
+            m = m & ~narrow
+        e = _bits(m)
+        k = 1
+        while k * 2 <= len(e) and PART % (k * 2) == 0:
+            k *= 2
+        return sum(1 << x for x in e[:k])
+
+    reps = {k: [] for k in range(n)}
+    hosted = {p: 0 for p in range(n)}
+    nodes = {0: {(r, r) for r in range(n)}, TIMES: {(r, r) for r in range(n)}}
+    for t in range(TIMES - 1, 0, -1):
+        nodes[t] = {(k, k) for k in range(n)}
+        if t not in LEVELS:
+            continue
+        far = {}
+        for (q, s) in sorted(nodes[t + 1]):
+            for k in tab[q]:
+                if k != s and not adj(k, s):
+                    far.setdefault(k, set()).add(s)
+        for k in sorted(far):
+            left = set(far[k])
+            for p in reps[k]:
+                cov = {s for s in left if s == p or adj(p, s)}
+                if cov:
+                    nodes[t].add((k, p))
+                    left -= cov
+            if not left:
+                continue
+
+            def score(p):
+                more = 0
+                if t - 1 in LEVELS:
+                    more = sum(1 for l in tab[k] if l != p and l != k and not adj(l, p)
+                               and not any(x == p or adj(x, p) for x in reps[l]))
+                link = sum(1 for a in range(n) for b in reps[a] if near(a, k) and near(b, p))
+                away = (sum(1 for r in range(n) if p in tab[r] and adj(p, r) and not near(r, p))
+                        + sum(1 for s in left if not near(p, s)))
+                new = sum(1 for l in tab[k] if l != k and l not in tab[p] and not near(l, p))
+                return (more, hosted[p], link, away, new, p)
+
+            p = min([p for p in range(n) if adj(k, p) and all(p == s or adj(p, s) for s in left)], key=score)
+            reps[k].append(p)
+            hosted[p] += 1
+            nodes[t].add((k, p))
+    assert max(hosted.values()) < NB
+    first_use = {}
+    for t in range(1, TIMES):
+        for (k, p) in sorted(nodes[t]):
+            if k != p:
+                first_use.setdefault((k, p), t)
+
+    out = {}
+    fwd = {}
+    sender = {}
+    hops = {}
+    load = {}
+    for t in range(TIMES):
+        need = {}
+        for (q, s) in sorted(nodes[t + 1]):
+            for k in tab[q]:
+                if (k, s) not in nodes[t]:
+                    need.setdefault(k, set()).add(s)
+        late = []
+        for k in sorted(need):
+            sites = sorted(p for (kk, p) in nodes[t] if kk == k)
+            for s in sorted(need[k]):
+                c = [p for p in sites if adj(p, s)]
+                if not c:
+                    late.append((k, s))
+                    continue
+                p = min(c, key=lambda p: (not near(p, s), load.get((t, p), 0), p != k, p))
+                out.setdefault((t, k, p), []).append(s)
+                sender[(t, k, s)] = p
+                hops[(t, k, s)] = 1
+                if not near(p, s):
+                    load[(t, p)] = load.get((t, p), 0) + 1
+        for (k, s) in late:
+            def cost(m):
+                has = (t, k, m) in sender and hops[(t, k, m)] == 1
+                duties = sum(len(d[1]) for d in fwd.get((t, m), []))
+                others = sum(1 for d in fwd.get((t, m), []) if d[0] != k)
+                busy = t == 0 and any(first_use[(m, p)] == 1 for p in reps[m])
+                return (not has, others, duties, busy, load.get((t, m), 0), m)
+
+            m = min([m for m in range(n) if adj(k, m) and adj(m, s)], key=cost)
+            if (t, k, m) not in sender:
+                out.setdefault((t, k, k), []).append(m)
+                sender[(t, k, m)] = k
+                hops[(t, k, m)] = 1
+                load[(t, k)] = load.get((t, k), 0) + 1
+            for d in fwd.setdefault((t, m), []):
+                if d[0] == k:
+                    d[1].append(s)
+                    break
+            else:
+                fwd[(t, m)].append([k, [s]])
+            sender[(t, k, s)] = m
+            hops[(t, k, s)] = 2
+            load[(t, m)] = load.get((t, m), 0) + 1
+
+    slots = {s: {} for s in range(n)}
+    for (t, k, s) in sorted(sender):
+        slots[s][(t, k)] = len(slots[s])
+    assert max(len(v) for v in slots.values()) <= NLAND
+    return {"nodes": nodes, "ships": reps, "first_use": first_use, "out": out, "fwd": fwd, "sender": sender, "hops": hops,
+            "slots": slots, "engines": engines, "near": near}
+
+
+def rank_program(g, core, T, topo):
+    me = T.rank_of(core)
+    if me is None:
+        return
+    cores, tab = list(T.cores), T.tables["MASK"]
+    if "plan" not in _CACHE:
+        _CACHE["plan"] = _plan(cores, tab, topo)
+    pl = _CACHE["plan"]
+    nodes, out, fwd, sender, hops, slots = pl["nodes"], pl["out"], pl["fwd"], pl["sender"], pl["hops"], pl["slots"]
+    engines, near = pl["engines"], pl["near"]
+    sem = T.sem
+    acc = [T.acc0, T.acc1]
+
+    def bank(j):
+        return 0 if j == me else 1
+
+    def mine(t, j):
+        c = 0 if t == 0 else 1 + (t - 1) * NB + bank(j)
+        return T.hb[:, c * TK:(c + 1) * TK]
+
+    def landed(s, t, j):
+        c = slots[s][(t, j)]
+        return T.land[:, c * TK:(c + 1) * TK]
+
+    def ready(t, j):
+        return (sem.xl, 16) if t == 0 else (sem["r%d_%d" % (t, bank(j))], 1)
+
+    def arrived(t, j):
+        return (sem["a%d_%d" % (t, j)], len(_bits(engines(sender[(t, j, me)], me))))
+
+    g.sync.dma_start(mine(0, me), T.x[:]).then_inc(sem.xl, 16)
+    g.sync.dma_start(T.ws[:, 0:DEG * PART], T.w[:]).then_inc(sem.wl, 16)
+    g.sync.wait_ge(*ready(TIMES, me))
+    g.sync.dma_start(T.y[:], mine(TIMES, me)).then_inc(sem.st, 16)
+    g.sync.wait_ge(sem.st, 16)
+
+    g.vector.memset(T.zero[:], 0.0).then_inc(sem.zs, 1)
+    g.vector.wait_ge(sem.zs, 1)
+    g.tensor.wait_ge(sem.wl, 16)
+    got_w = set()
+    order = {0: [me]}
+    for t in range(1, TIMES + 1):
+        here = sorted((j for (j, p) in nodes[t] if p == me), key=lambda j: (j != me, j))
+        terms = []
+        for j in here:
+            for i, k in enumerate(tab[j]):
+                if (k, me) in nodes[t - 1]:
+                    cls = 0
+                else:
+                    cls = (1 if near(sender[(t - 1, k, me)], me) else 2) + 2 * (hops[(t - 1, k, me)] - 1)
+                terms.append((cls, bank(j), i, j, k))
+        fresh = any(pl["first_use"].get((j, me)) == t for j in here)
+        terms.sort(key=lambda x: (x[1], x) if fresh else (0, x))
+        last = {j: [x for x in terms if x[3] == j][-1] for j in here}
+        begun = set()
+        for x in terms:
+            cls, b, i, j, k = x
+            if j != me and j not in got_w:
+                g.tensor.wait_ge(sem["wa%d" % j], len(_bits(engines(j, me))))
+                got_w.add(j)
+            if j not in begun and (j, me) in nodes[t - 1] and t > 1:
+                g.tensor.wait_ge(*ready(t - 1, j))
+            if cls == 0:
+                g.tensor.wait_ge(*ready(t - 1, k))
+                rhs = mine(t - 1, k)
+            else:
+                g.tensor.wait_ge(*arrived(t - 1, k))
+                rhs = landed(me, t - 1, k)
+            c = (b * DEG + i) * PART
+            mm = g.tensor.matmul(acc[b][:, 0:TK], T.ws[:, c:c + PART], rhs, j not in begun, x == last[j])
+            begun.add(j)
+            if x == last[j]:
+                mm.then_inc(sem["m%d_%d" % (t, b)], 1)
+        order[t] = sorted(here, key=lambda j: terms.index(last[j]))
+        for j in order[t]:
+            g.vector.wait_ge(sem["m%d_%d" % (t, bank(j))], 1)
+            g.vector.tensor_tensor(mine(t, j), acc[bank(j)][:, 0:TK], T.zero[:], AluOpType.max).then_inc(ready(t, j)[0], 1)
+
+    sent = [0]
+
+    def send(src, t, j, dests):
+        groups = {}
+        for d in dests:
+            groups.setdefault(engines(me, d), []).append(d)
+        trs = []
+        for m in sorted(groups):
+            ids = []
+            for d in groups[m]:
+                rid, pid = topo.addr(cores[d], core)
+                ids.append(DstId(rid=rid, pnc=pid))
+            trs.append(RemoteDMATransfer(dst_ids=ids, dma_engine_mask=m, remote_sem=sem["a%d_%d" % (t, j)], srcs=[src],
+                                         dsts=[landed(d, t, j) for d in groups[m]], alu_op=0))
+            sent[0] += len(_bits(m))
+        g.remote_dma_fused(trs, local_sem=sem.sent)
+
+    def ship(early):
+        for p in pl["ships"][me]:
+            if (pl["first_use"][(me, p)] == 1) == early:
+                g.wait_ge(sem.wl, 16)
+                rid, pid = topo.addr(cores[p], core)
+                m = engines(me, p)
+                g.remote_dma(T.ws[:, DEG * PART:2 * DEG * PART], T.ws[:, 0:DEG * PART], sem["wa%d" % me], sem.sent, pid, rid, m)
+                sent[0] += len(_bits(m))
+
+    for t in range(TIMES):
+        for j in order[t]:
+            dests = out.get((t, j, me), [])
+            urgent = [d for d in dests if any(x[0] == j for x in fwd.get((t, d), []))]
+            rest = [d for d in dests if d not in urgent]
+            if dests:
+                g.wait_ge(*ready(t, j))
+            if urgent:
+                send(mine(t, j), t, j, urgent)
+            if t == 0:
+                ship(True)
+            if rest:
+                send(mine(t, j), t, j, rest)
+        for (k, dests) in fwd.get((t, me), []):
+            g.wait_ge(*arrived(t, k))
+            send(landed(me, t, k), t, k, dests)
+        if t == 0:
+            ship(False)
+    g.wait_ge(sem.sent, sent[0])

@@ -2,23 +2,19 @@ from concourse.bass import DstId, RemoteDMATransfer
 from concourse.mybir import AluOpType
 
 PART, TK, DEG, TIMES, NR = 128, 64, 4, 3, 16
-LEVELS = (1, 2)
-NB = 2
-NLAND = 16
+NLAND = 6
 
 SCRATCH = {
-    "hb": ("sbuf", [PART, (1 + TIMES * NB) * TK], "bfloat16"),
-    "ws": ("sbuf", [PART, NB * DEG * PART], "bfloat16"),
-    "land": ("sbuf", [PART, NLAND * TK], "bfloat16"),
+    "hb": ("sbuf", [PART, (1 + TIMES) * TK], "bfloat16"),
+    "ws": ("sbuf", [PART, DEG * PART], "bfloat16"),
+    "land": ("sbuf", [PART, TIMES * NLAND * TK], "bfloat16"),
     "zero": ("sbuf", [PART, TK], "float32"),
     "acc0": ("psum", [PART, 512], "float32"),
-    "acc1": ("psum", [PART, 512], "float32"),
 }
 SEMAPHORES = (["xl", "wl", "zs", "sent", "st"]
-              + ["m%d_%d" % (t, b) for t in range(1, TIMES + 1) for b in range(NB)]
-              + ["r%d_%d" % (t, b) for t in range(1, TIMES + 1) for b in range(NB)]
-              + ["a%d_%d" % (t, j) for t in range(TIMES) for j in range(NR)]
-              + ["wa%d" % j for j in range(NR)])
+              + ["m%d" % t for t in range(1, TIMES + 1)]
+              + ["r%d" % t for t in range(1, TIMES + 1)]
+              + ["a%d_%d" % (t, j) for t in range(TIMES) for j in range(NR)])
 
 _CACHE = {}
 
@@ -33,8 +29,11 @@ def _plan(cores, tab, topo):
     def adj(a, b):
         return a != b and topo.may_write(cores[a], cores[b])
 
+    def place(a):
+        return (topo.host(cores[a]), topo.chip(cores[a]))
+
     def near(a, b):
-        return topo.host(cores[a]) == topo.host(cores[b]) and topo.chip(cores[a]) == topo.chip(cores[b])
+        return place(a) == place(b)
 
     def engines(a, b):
         narrow = 0
@@ -51,105 +50,87 @@ def _plan(cores, tab, topo):
             k *= 2
         return sum(1 << x for x in e[:k])
 
-    reps = {k: [] for k in range(n)}
-    hosted = {p: 0 for p in range(n)}
-    nodes = {0: {(r, r) for r in range(n)}, TIMES: {(r, r) for r in range(n)}}
-    for t in range(TIMES - 1, 0, -1):
-        nodes[t] = {(k, k) for k in range(n)}
-        if t not in LEVELS:
-            continue
-        far = {}
-        for (q, s) in sorted(nodes[t + 1]):
-            for k in tab[q]:
-                if k != s and not adj(k, s):
-                    far.setdefault(k, set()).add(s)
-        for k in sorted(far):
-            left = set(far[k])
-            for p in reps[k]:
-                cov = {s for s in left if s == p or adj(p, s)}
-                if cov:
-                    nodes[t].add((k, p))
-                    left -= cov
-            if not left:
-                continue
-
-            def score(p):
-                more = 0
-                if t - 1 in LEVELS:
-                    more = sum(1 for l in tab[k] if l != p and l != k and not adj(l, p)
-                               and not any(x == p or adj(x, p) for x in reps[l]))
-                link = sum(1 for a in range(n) for b in reps[a] if near(a, k) and near(b, p))
-                away = (sum(1 for r in range(n) if p in tab[r] and adj(p, r) and not near(r, p))
-                        + sum(1 for s in left if not near(p, s)))
-                new = sum(1 for l in tab[k] if l != k and l not in tab[p] and not near(l, p))
-                return (more, hosted[p], link, away, new, p)
-
-            p = min([p for p in range(n) if adj(k, p) and all(p == s or adj(p, s) for s in left)], key=score)
-            reps[k].append(p)
-            hosted[p] += 1
-            nodes[t].add((k, p))
-    assert max(hosted.values()) < NB
-    first_use = {}
-    for t in range(1, TIMES):
-        for (k, p) in sorted(nodes[t]):
-            if k != p:
-                first_use.setdefault((k, p), t)
-
-    out = {}
-    fwd = {}
-    sender = {}
-    hops = {}
-    load = {}
-    for t in range(TIMES):
-        need = {}
-        for (q, s) in sorted(nodes[t + 1]):
-            for k in tab[q]:
-                if (k, s) not in nodes[t]:
-                    need.setdefault(k, set()).add(s)
-        late = []
-        for k in sorted(need):
-            sites = sorted(p for (kk, p) in nodes[t] if kk == k)
-            for s in sorted(need[k]):
-                c = [p for p in sites if adj(p, s)]
-                if not c:
-                    late.append((k, s))
-                    continue
-                p = min(c, key=lambda p: (not near(p, s), load.get((t, p), 0), p != k, p))
-                out.setdefault((t, k, p), []).append(s)
-                sender[(t, k, s)] = p
-                hops[(t, k, s)] = 1
-                if not near(p, s):
-                    load[(t, p)] = load.get((t, p), 0) + 1
-        for (k, s) in late:
-            def cost(m):
-                has = (t, k, m) in sender and hops[(t, k, m)] == 1
-                duties = sum(len(d[1]) for d in fwd.get((t, m), []))
-                others = sum(1 for d in fwd.get((t, m), []) if d[0] != k)
-                busy = t == 0 and any(first_use[(m, p)] == 1 for p in reps[m])
-                return (not has, others, duties, busy, load.get((t, m), 0), m)
-
-            m = min([m for m in range(n) if adj(k, m) and adj(m, s)], key=cost)
-            if (t, k, m) not in sender:
-                out.setdefault((t, k, k), []).append(m)
-                sender[(t, k, m)] = k
-                hops[(t, k, m)] = 1
-                load[(t, k)] = load.get((t, k), 0) + 1
-            for d in fwd.setdefault((t, m), []):
-                if d[0] == k:
-                    d[1].append(s)
-                    break
+    need = {}
+    for q in range(n):
+        for k in tab[q]:
+            if k != q:
+                need.setdefault(k, set()).add(q)
+    groups, local, late = {}, {}, []
+    for k in sorted(need):
+        for s in sorted(need[k]):
+            if near(k, s):
+                local.setdefault(k, []).append(s)
+            elif adj(k, s):
+                groups.setdefault((k, place(s)), []).append(s)
             else:
-                fwd[(t, m)].append([k, [s]])
-            sender[(t, k, s)] = m
-            hops[(t, k, s)] = 2
-            load[(t, m)] = load.get((t, m), 0) + 1
+                late.append((k, s))
+    link, away, duty = {}, {}, {}
+    for (k, P) in groups:
+        link[(place(k), P)] = link.get((place(k), P), 0) + 1
+        away[k] = away.get(k, 0) + 1
+    prim, relay = {}, {}
 
+    def pick(k, P):
+        if (k, P) in prim:
+            return prim[(k, P)]
+        c = groups.get((k, P))
+        if c is None:
+            c = [m for m in range(n) if place(m) == P and adj(k, m)]
+        return min(c, key=lambda m: (duty.get(m, 0), away.get(m, 0), m))
+
+    for (k, s) in late:
+        best = None
+        for P in sorted({place(m) for m in range(n) if adj(k, m) and adj(m, s) and not near(k, m)}):
+            m = pick(k, P)
+            feed = 0 if (k, P) in groups else 1
+            l2 = link.get((P, place(s)), 0) + 1
+            l1 = link.get((place(k), P), 0) + feed
+            sc = (max(l2, l1 if feed else 0, away.get(m, 0) + 1), feed, l2, m)
+            if best is None or sc < best[0]:
+                best = (sc, P, m, feed)
+        sc, P, m, feed = best
+        if feed:
+            groups[(k, P)] = [m]
+            link[(place(k), P)] = link.get((place(k), P), 0) + 1
+            away[k] = away.get(k, 0) + 1
+        prim.setdefault((k, P), m)
+        if (k, m) not in relay:
+            duty[m] = duty.get(m, 0) + 1
+        relay.setdefault((k, m), []).append(s)
+        link[(P, place(s))] = link.get((P, place(s)), 0) + 1
+        away[m] = away.get(m, 0) + 1
+    for (k, P) in sorted(groups):
+        if (k, P) not in prim:
+            m = pick(k, P)
+            prim[(k, P)] = m
+            if len(groups[(k, P)]) > 1:
+                duty[m] = duty.get(m, 0) + 1
+
+    first, rest, fwd, sender, hops = {}, {}, {}, {}, {}
+    for (k, P) in sorted(groups):
+        m = prim[(k, P)]
+        sender[(k, m)], hops[(k, m)] = k, 1
+        far = relay.get((k, m), [])
+        dests = far + [s for s in groups[(k, P)] if s != m]
+        if dests:
+            first.setdefault(k, []).append(m)
+            fwd.setdefault(m, []).append((0 if far else 1, k, dests))
+            for s in dests:
+                sender[(k, s)], hops[(k, s)] = m, 2
+        else:
+            rest.setdefault(k, []).append(m)
+    for k in sorted(local):
+        for s in local[k]:
+            rest.setdefault(k, []).append(s)
+            sender[(k, s)], hops[(k, s)] = k, 1
+    for m in fwd:
+        fwd[m].sort()
     slots = {s: {} for s in range(n)}
-    for (t, k, s) in sorted(sender):
-        slots[s][(t, k)] = len(slots[s])
+    for (k, s) in sorted(sender):
+        slots[s][k] = len(slots[s])
     assert max(len(v) for v in slots.values()) <= NLAND
-    return {"nodes": nodes, "ships": reps, "first_use": first_use, "out": out, "fwd": fwd, "sender": sender, "hops": hops,
-            "slots": slots, "engines": engines, "near": near}
+    return {"first": first, "rest": rest, "fwd": fwd, "sender": sender, "hops": hops, "slots": slots, "engines": engines,
+            "near": near}
 
 
 def rank_program(g, core, T, topo):
@@ -160,75 +141,51 @@ def rank_program(g, core, T, topo):
     if "plan" not in _CACHE:
         _CACHE["plan"] = _plan(cores, tab, topo)
     pl = _CACHE["plan"]
-    nodes, out, fwd, sender, hops, slots = pl["nodes"], pl["out"], pl["fwd"], pl["sender"], pl["hops"], pl["slots"]
-    engines, near = pl["engines"], pl["near"]
+    sender, hops, slots, engines, near = pl["sender"], pl["hops"], pl["slots"], pl["engines"], pl["near"]
     sem = T.sem
-    acc = [T.acc0, T.acc1]
 
-    def bank(j):
-        return 0 if j == me else 1
-
-    def mine(t, j):
-        c = 0 if t == 0 else 1 + (t - 1) * NB + bank(j)
-        return T.hb[:, c * TK:(c + 1) * TK]
+    def mine(t):
+        return T.hb[:, t * TK:(t + 1) * TK]
 
     def landed(s, t, j):
-        c = slots[s][(t, j)]
+        c = t * NLAND + slots[s][j]
         return T.land[:, c * TK:(c + 1) * TK]
 
-    def ready(t, j):
-        return (sem.xl, 16) if t == 0 else (sem["r%d_%d" % (t, bank(j))], 1)
+    def ready(t):
+        return (sem.xl, 16) if t == 0 else (sem["r%d" % t], 1)
 
     def arrived(t, j):
-        return (sem["a%d_%d" % (t, j)], len(_bits(engines(sender[(t, j, me)], me))))
+        return (sem["a%d_%d" % (t, j)], len(_bits(engines(sender[(j, me)], me))))
 
-    g.sync.dma_start(mine(0, me), T.x[:]).then_inc(sem.xl, 16)
-    g.sync.dma_start(T.ws[:, 0:DEG * PART], T.w[:]).then_inc(sem.wl, 16)
-    g.sync.wait_ge(*ready(TIMES, me))
-    g.sync.dma_start(T.y[:], mine(TIMES, me)).then_inc(sem.st, 16)
+    g.sync.dma_start(mine(0), T.x[:]).then_inc(sem.xl, 16)
+    g.sync.dma_start(T.ws[:], T.w[:]).then_inc(sem.wl, 16)
+    g.sync.wait_ge(*ready(TIMES))
+    g.sync.dma_start(T.y[:], mine(TIMES)).then_inc(sem.st, 16)
     g.sync.wait_ge(sem.st, 16)
 
     g.vector.memset(T.zero[:], 0.0).then_inc(sem.zs, 1)
     g.vector.wait_ge(sem.zs, 1)
     g.tensor.wait_ge(sem.wl, 16)
-    got_w = set()
-    order = {0: [me]}
+    terms = []
+    for i, k in enumerate(tab[me]):
+        cls = 0 if k == me else (1 if near(sender[(k, me)], me) else 2) + 2 * (hops[(k, me)] - 1)
+        terms.append((cls, i, k))
+    terms.sort()
+    assert terms[0][0] == 0
     for t in range(1, TIMES + 1):
-        here = sorted((j for (j, p) in nodes[t] if p == me), key=lambda j: (j != me, j))
-        terms = []
-        for j in here:
-            for i, k in enumerate(tab[j]):
-                if (k, me) in nodes[t - 1]:
-                    cls = 0
-                else:
-                    cls = (1 if near(sender[(t - 1, k, me)], me) else 2) + 2 * (hops[(t - 1, k, me)] - 1)
-                terms.append((cls, bank(j), i, j, k))
-        fresh = any(pl["first_use"].get((j, me)) == t for j in here)
-        terms.sort(key=lambda x: (x[1], x) if fresh else (0, x))
-        last = {j: [x for x in terms if x[3] == j][-1] for j in here}
-        begun = set()
         for x in terms:
-            cls, b, i, j, k = x
-            if j != me and j not in got_w:
-                g.tensor.wait_ge(sem["wa%d" % j], len(_bits(engines(j, me))))
-                got_w.add(j)
-            if j not in begun and (j, me) in nodes[t - 1] and t > 1:
-                g.tensor.wait_ge(*ready(t - 1, j))
+            cls, i, k = x
             if cls == 0:
-                g.tensor.wait_ge(*ready(t - 1, k))
-                rhs = mine(t - 1, k)
+                g.tensor.wait_ge(*ready(t - 1))
+                rhs = mine(t - 1)
             else:
                 g.tensor.wait_ge(*arrived(t - 1, k))
                 rhs = landed(me, t - 1, k)
-            c = (b * DEG + i) * PART
-            mm = g.tensor.matmul(acc[b][:, 0:TK], T.ws[:, c:c + PART], rhs, j not in begun, x == last[j])
-            begun.add(j)
-            if x == last[j]:
-                mm.then_inc(sem["m%d_%d" % (t, b)], 1)
-        order[t] = sorted(here, key=lambda j: terms.index(last[j]))
-        for j in order[t]:
-            g.vector.wait_ge(sem["m%d_%d" % (t, bank(j))], 1)
-            g.vector.tensor_tensor(mine(t, j), acc[bank(j)][:, 0:TK], T.zero[:], AluOpType.max).then_inc(ready(t, j)[0], 1)
+            mm = g.tensor.matmul(T.acc0[:, 0:TK], T.ws[:, i * PART:(i + 1) * PART], rhs, x == terms[0], x == terms[-1])
+            if x == terms[-1]:
+                mm.then_inc(sem["m%d" % t], 1)
+        g.vector.wait_ge(sem["m%d" % t], 1)
+        g.vector.tensor_tensor(mine(t), T.acc0[:, 0:TK], T.zero[:], AluOpType.max).then_inc(sem["r%d" % t], 1)
 
     sent = [0]
 
@@ -247,31 +204,13 @@ def rank_program(g, core, T, topo):
             sent[0] += len(_bits(m))
         g.remote_dma_fused(trs, local_sem=sem.sent)
 
-    def ship(early):
-        for p in pl["ships"][me]:
-            if (pl["first_use"][(me, p)] == 1) == early:
-                g.wait_ge(sem.wl, 16)
-                rid, pid = topo.addr(cores[p], core)
-                m = engines(me, p)
-                g.remote_dma(T.ws[:, DEG * PART:2 * DEG * PART], T.ws[:, 0:DEG * PART], sem["wa%d" % me], sem.sent, pid, rid, m)
-                sent[0] += len(_bits(m))
-
     for t in range(TIMES):
-        for j in order[t]:
-            dests = out.get((t, j, me), [])
-            urgent = [d for d in dests if any(x[0] == j for x in fwd.get((t, d), []))]
-            rest = [d for d in dests if d not in urgent]
-            if dests:
-                g.wait_ge(*ready(t, j))
-            if urgent:
-                send(mine(t, j), t, j, urgent)
-            if t == 0:
-                ship(True)
-            if rest:
-                send(mine(t, j), t, j, rest)
-        for (k, dests) in fwd.get((t, me), []):
+        g.wait_ge(*ready(t))
+        if pl["first"].get(me):
+            send(mine(t), t, me, pl["first"][me])
+        if pl["rest"].get(me):
+            send(mine(t), t, me, pl["rest"][me])
+        for (_, k, dests) in pl["fwd"].get(me, []):
             g.wait_ge(*arrived(t, k))
             send(landed(me, t, k), t, k, dests)
-        if t == 0:
-            ship(False)
     g.wait_ge(sem.sent, sent[0])

from concourse.bass import DstId, RemoteDMATransfer
from concourse.mybir import AluOpType

PART, TK, DEG, TIMES, NR = 128, 64, 4, 3, 16
NLAND = 6

SCRATCH = {
    "hb": ("sbuf", [PART, (1 + TIMES) * TK], "bfloat16"),
    "ws": ("sbuf", [PART, DEG * PART], "bfloat16"),
    "land": ("sbuf", [PART, TIMES * NLAND * TK], "bfloat16"),
    "zero": ("sbuf", [PART, TK], "float32"),
    "acc0": ("psum", [PART, 512], "float32"),
}
SEMAPHORES = (["xl", "wl", "zs", "sent", "st"]
              + ["m%d" % t for t in range(1, TIMES + 1)]
              + ["r%d" % t for t in range(1, TIMES + 1)]
              + ["a%d_%d" % (t, j) for t in range(TIMES) for j in range(NR)])

_CACHE = {}


def _bits(m):
    return [e for e in range(m.bit_length()) if (m >> e) & 1]


def _plan(cores, tab, topo):
    n = len(cores)

    def adj(a, b):
        return a != b and topo.may_write(cores[a], cores[b])

    def place(a):
        return (topo.host(cores[a]), topo.chip(cores[a]))

    def near(a, b):
        return place(a) == place(b)

    def engines(a, b):
        narrow = 0
        for c in range(n):
            if adj(a, c):
                m = topo.mask(cores[a], cores[c])
                narrow = m if narrow == 0 else narrow & m
        m = topo.mask(cores[a], cores[b])
        if m != narrow and m & ~narrow:
            m = m & ~narrow
        e = _bits(m)
        k = 1
        while k * 2 <= len(e) and PART % (k * 2) == 0:
            k *= 2
        return sum(1 << x for x in e[:k])

    need = {}
    for q in range(n):
        for k in tab[q]:
            if k != q:
                need.setdefault(k, set()).add(q)
    groups, local, late = {}, {}, []
    for k in sorted(need):
        for s in sorted(need[k]):
            if near(k, s):
                local.setdefault(k, []).append(s)
            elif adj(k, s):
                groups.setdefault((k, place(s)), []).append(s)
            else:
                late.append((k, s))
    link, away, duty = {}, {}, {}
    for (k, P) in groups:
        link[(place(k), P)] = link.get((place(k), P), 0) + 1
        away[k] = away.get(k, 0) + 1
    prim, relay = {}, {}

    def pick(k, P):
        if (k, P) in prim:
            return prim[(k, P)]
        c = groups.get((k, P))
        if c is None:
            c = [m for m in range(n) if place(m) == P and adj(k, m)]
        return min(c, key=lambda m: (duty.get(m, 0), away.get(m, 0), m))

    for (k, s) in late:
        best = None
        for P in sorted({place(m) for m in range(n) if adj(k, m) and adj(m, s) and not near(k, m)}):
            m = pick(k, P)
            feed = 0 if (k, P) in groups else 1
            l2 = link.get((P, place(s)), 0) + 1
            l1 = link.get((place(k), P), 0) + feed
            sc = (max(l2, l1 if feed else 0, away.get(m, 0) + 1), feed, l2, m)
            if best is None or sc < best[0]:
                best = (sc, P, m, feed)
        sc, P, m, feed = best
        if feed:
            groups[(k, P)] = [m]
            link[(place(k), P)] = link.get((place(k), P), 0) + 1
            away[k] = away.get(k, 0) + 1
        prim.setdefault((k, P), m)
        if (k, m) not in relay:
            duty[m] = duty.get(m, 0) + 1
        relay.setdefault((k, m), []).append(s)
        link[(P, place(s))] = link.get((P, place(s)), 0) + 1
        away[m] = away.get(m, 0) + 1
    for (k, P) in sorted(groups):
        if (k, P) not in prim:
            m = pick(k, P)
            prim[(k, P)] = m
            if len(groups[(k, P)]) > 1:
                duty[m] = duty.get(m, 0) + 1

    first, rest, fwd, sender, hops = {}, {}, {}, {}, {}
    for (k, P) in sorted(groups):
        m = prim[(k, P)]
        sender[(k, m)], hops[(k, m)] = k, 1
        far = relay.get((k, m), [])
        dests = far + [s for s in groups[(k, P)] if s != m]
        if dests:
            first.setdefault(k, []).append(m)
            fwd.setdefault(m, []).append((0 if far else 1, k, dests))
            for s in dests:
                sender[(k, s)], hops[(k, s)] = m, 2
        else:
            rest.setdefault(k, []).append(m)
    for k in sorted(local):
        for s in local[k]:
            rest.setdefault(k, []).append(s)
            sender[(k, s)], hops[(k, s)] = k, 1
    for m in fwd:
        fwd[m].sort()
    slots = {s: {} for s in range(n)}
    for (k, s) in sorted(sender):
        slots[s][k] = len(slots[s])
    assert max(len(v) for v in slots.values()) <= NLAND
    return {"first": first, "rest": rest, "fwd": fwd, "sender": sender, "hops": hops, "slots": slots, "engines": engines,
            "near": near}


def rank_program(g, core, T, topo):
    me = T.rank_of(core)
    if me is None:
        return
    cores, tab = list(T.cores), T.tables["MASK"]
    if "plan" not in _CACHE:
        _CACHE["plan"] = _plan(cores, tab, topo)
    pl = _CACHE["plan"]
    sender, hops, slots, engines, near = pl["sender"], pl["hops"], pl["slots"], pl["engines"], pl["near"]
    sem = T.sem

    def mine(t):
        return T.hb[:, t * TK:(t + 1) * TK]

    def landed(s, t, j):
        c = t * NLAND + slots[s][j]
        return T.land[:, c * TK:(c + 1) * TK]

    def ready(t):
        return (sem.xl, 16) if t == 0 else (sem["r%d" % t], 1)

    def arrived(t, j):
        return (sem["a%d_%d" % (t, j)], len(_bits(engines(sender[(j, me)], me))))

    g.sync.dma_start(mine(0), T.x[:]).then_inc(sem.xl, 16)
    g.sync.dma_start(T.ws[:], T.w[:]).then_inc(sem.wl, 16)
    g.sync.wait_ge(*ready(TIMES))
    g.sync.dma_start(T.y[:], mine(TIMES)).then_inc(sem.st, 16)
    g.sync.wait_ge(sem.st, 16)

    g.vector.memset(T.zero[:], 0.0).then_inc(sem.zs, 1)
    g.vector.wait_ge(sem.zs, 1)
    g.tensor.wait_ge(sem.wl, 16)
    terms = []
    for i, k in enumerate(tab[me]):
        cls = 0 if k == me else (1 if near(sender[(k, me)], me) else 2) + 2 * (hops[(k, me)] - 1)
        terms.append((cls, i, k))
    terms.sort()
    assert terms[0][0] == 0
    for t in range(1, TIMES + 1):
        for x in terms:
            cls, i, k = x
            if cls == 0:
                g.tensor.wait_ge(*ready(t - 1))
                rhs = mine(t - 1)
            else:
                g.tensor.wait_ge(*arrived(t - 1, k))
                rhs = landed(me, t - 1, k)
            mm = g.tensor.matmul(T.acc0[:, 0:TK], T.ws[:, i * PART:(i + 1) * PART], rhs, x == terms[0], x == terms[-1])
            if x == terms[-1]:
                mm.then_inc(sem["m%d" % t], 1)
        g.vector.wait_ge(sem["m%d" % t], 1)
        g.vector.tensor_tensor(mine(t), T.acc0[:, 0:TK], T.zero[:], AluOpType.max).then_inc(sem["r%d" % t], 1)

    sent = [0]

    def send(src, t, j, dests):
        groups = {}
        for d in dests:
            groups.setdefault(engines(me, d), []).append(d)
        trs = []
        for m in sorted(groups):
            ids = []
            for d in groups[m]:
                rid, pid = topo.addr(cores[d], core)
                ids.append(DstId(rid=rid, pnc=pid))
            trs.append(RemoteDMATransfer(dst_ids=ids, dma_engine_mask=m, remote_sem=sem["a%d_%d" % (t, j)], srcs=[src],
                                         dsts=[landed(d, t, j) for d in groups[m]], alu_op=0))
            sent[0] += len(_bits(m))
        g.remote_dma_fused(trs, local_sem=sem.sent)

    for t in range(TIMES):
        g.wait_ge(*ready(t))
        if pl["first"].get(me):
            send(mine(t), t, me, pl["first"][me])
        if pl["rest"].get(me):
            send(mine(t), t, me, pl["rest"][me])
        for (_, k, dests) in pl["fwd"].get(me, []):
            g.wait_ge(*arrived(t, k))
            send(landed(me, t, k), t, k, dests)
    g.wait_ge(sem.sent, sent[0])
